import numpy as np
import ml_dtypes


def mxq(x, axis, fmt="e4m3"):
    dtype, down = {"e4m3": (ml_dtypes.float8_e4m3fn, 7), "e5m2": (ml_dtypes.float8_e5m2, 14)}[fmt]
    v = np.moveaxis(np.asarray(x, np.float32).astype(ml_dtypes.bfloat16).astype(np.float64), axis, -1)
    blocks = v.reshape(v.shape[:-1] + (-1, 32))
    amax = np.abs(blocks).max(-1, keepdims=True)
    byte = np.maximum(np.where(amax > 0, np.frexp(amax)[1] - 1 + 127, 0) - down, 1)
    scale = np.exp2(byte - 127.0)
    codes = (blocks / scale).astype(np.float32).astype(dtype).astype(np.float64)
    return np.moveaxis((codes * scale).reshape(v.shape), -1, axis)


WIDE = False


def mx_kscale(k):
    if not WIDE:
        return np.ones(k)
    levels = np.array([10, -10, 5, -5, 0])
    if k % 512:
        return np.exp2(np.random.permutation(np.resize(levels, k // 32))).repeat(32)
    a = np.empty((k // 512, 16))
    for p in range(k // 512):
        a[p, :8] = np.random.permutation(np.resize(levels, 8))
        for g in range(8):
            far = levels[np.abs(levels - a[p, g]) >= 10]
            a[p, g + 8] = far[np.random.randint(len(far))]
    return np.exp2(a.ravel()).repeat(32)


def f64(x):
    return np.asarray(x).astype(np.float64)


def striped(idx):
    return np.tile(np.asarray(idx).reshape(-1, 16).T, (8, 1)).astype(np.uint16)


def unstriped(offs):
    return offs[:16].T.reshape(-1).astype(np.int64)


E2M1 = np.array([0.0, 0.5, 1.0, 1.5, 2.0, 3.0, 4.0, 6.0, -0.0, -0.5, -1.0, -1.5, -2.0, -3.0, -4.0, -6.0])


def pack_weight(w, fmt):
    k, n = w.shape
    w = f64(np.asarray(w, np.float32).astype(ml_dtypes.bfloat16)).reshape(k // 32, 32, n)
    amax = np.abs(w).max(1)
    if fmt == "e4m3":
        byte = np.frexp(amax)[1] - 1 + 127 - 7
    else:
        mant, ex = np.frexp(amax / 6.0)
        byte = np.where(mant > 0.5, ex, ex - 1) + 127
    byte = np.clip(np.where(amax > 0, byte, 1), 1, 254)
    scaled = (w * np.exp2(127.0 - byte)[:, None, :]).reshape(k, n).astype(np.float32)
    by_word = np.ascontiguousarray(scaled.reshape(k // 512, 128, 4, n).transpose(0, 1, 3, 2))
    if fmt == "e4m3":
        words = by_word.astype(ml_dtypes.float8_e4m3fn).view(np.uint8)
    else:
        c = by_word.astype(ml_dtypes.float4_e2m1fn).view(np.uint8) & 0xF
        words = (c[..., 0::2] | (c[..., 1::2] << 4)).reshape(k // 512, 128, 2 * n)
    return np.ascontiguousarray(words), np.ascontiguousarray(byte.astype(np.uint8).reshape(k // 512, 16, n))


def unpack_weight(words, scales, fmt):
    g, _, n = scales.shape
    words = np.ascontiguousarray(words).reshape(g, 128, n, -1)
    if fmt == "e4m3":
        vals = words.view(ml_dtypes.float8_e4m3fn).astype(np.float64)
    else:
        nib = np.empty((g, 128, n, 4), np.uint8)
        nib[..., 0::2] = words & 0xF
        nib[..., 1::2] = words >> 4
        vals = E2M1[nib]
    vals = vals * np.repeat(np.exp2(scales.astype(np.float64) - 127.0), 8, axis=1)[..., None]
    return vals.transpose(0, 1, 3, 2).reshape(g * 512, n)


D, K, T, I, Q = 1024, 512, 2048, 512, 128


def setup_inputs():
    n = np.random.standard_normal
    idx = np.random.permutation(T)[:I]
    fd = mx_kscale(D)
    fk = mx_kscale(K)
    etp = pack_weight(n((D, T)) / fd[:, None], "e2m1")
    edp = pack_weight(n((K, T)) / fk[:, None], "e4m3")
    return {
        "ht": (n((D, Q)) * 1.0 / np.sqrt(D) * fd[:, None]).astype(np.float32),
        "hd": (n((K, Q)) * 1.0 / np.sqrt(K) * fk[:, None]).astype(np.float32),
        "et_words": etp[0],
        "et_scales": etp[1],
        "ed_words": edp[0],
        "ed_scales": edp[1],
        "l1": (np.random.uniform(6.6, 6.9, (Q, 1))).astype(np.float32),
        "l2": (np.random.uniform(6.6, 6.9, (Q, 1))).astype(np.float32),
        "offs": striped(idx),
    }


def reference(ht, hd, et_words, et_scales, ed_words, ed_scales, l1, l2, offs):
    idx = unstriped(offs)
    etu = unpack_weight(et_words, et_scales, "e2m1")
    edu = unpack_weight(ed_words, ed_scales, "e4m3")
    htq = mxq(f64(ht), 0, "e4m3")
    etidxg = etu[:, idx]
    a = htq.T @ etidxg
    hdq = mxq(f64(hd), 0, "e4m3")
    edidxg = edu[:, idx]
    b = hdq.T @ edidxg
    p = np.maximum(np.exp(a - f64(l1)) - np.exp(b - f64(l2)), 0.0)
    y = p / np.sum(p, axis=1, keepdims=True) * 512.0
    return y

@@ -1,0 +1,145 @@
+from contextlib import ExitStack
+
+import concourse.mybir as mybir
+
+D, K, T, I, Q = 1024, 512, 2048, 512, 128
+FLOPS = 2 * Q * I * (D + K)
+
+F32 = mybir.dt.float32
+BF16 = mybir.dt.bfloat16
+I32 = mybir.dt.int32
+U32 = mybir.dt.uint32
+U16 = mybir.dt.uint16
+U8 = mybir.dt.uint8
+FP8X4 = mybir.dt.float8_e4m3fn_x4
+FP4X4 = mybir.dt.float4_e2m1fn_x4
+ALU = mybir.AluOpType
+ACT = mybir.ActivationFunctionType
+
+P = 128
+PACK = 4
+HALF = I // 2
+SHIFT = 16
+ED_ROW = 4
+
+
+def tile_attend_speculate_residual_kernel(tc, ht, hd, et_words, et_scales, ed_words, ed_scales, l1, l2, offs, out):
+    nc = tc.nc
+    with ExitStack() as ctx:
+        keep = ctx.enter_context(tc.tile_pool(name="keep", bufs=1))
+        psum = ctx.enter_context(tc.psum_pool(name="psum", bufs=1))
+
+        offsets = keep.tile([P, I // 16], U16, name="offsets")
+        et_win = [keep.tile([P, T], U16, name=f"et_win{z}", align_bytes=64) for z in range(2)]
+        ed_win = keep.tile([P, T], U32, name="ed_win", align_bytes=64)
+        ets_win = keep.tile([P, T], U8, name="ets_win", align_bytes=64)
+        eds_win = keep.tile([P, T], U8, name="eds_win", align_bytes=64)
+        et_g = [keep.tile([P, I], U16, name=f"et_g{z}", align_bytes=64) for z in range(2)]
+        ed_g = [keep.tile([P, HALF], U32, name=f"ed_g{h}", align_bytes=64) for h in range(2)]
+        ets_g = keep.tile([P, I], U8, name="ets_g", align_bytes=64)
+        ets_1 = keep.tile([P, I], U8, name="ets_1", align_bytes=64)
+        eds_g = keep.tile([P, I], U8, name="eds_g", align_bytes=64)
+        ht_raw = keep.tile([P, 2, PACK, Q], F32, name="ht_raw", align_bytes=64)
+        hd_raw = keep.tile([P, PACK, Q], F32, name="hd_raw", align_bytes=64)
+        ht_bf = keep.tile([P, 2, Q, PACK], BF16, name="ht_bf", align_bytes=64)
+        hd_bf = keep.tile([P, Q, PACK], BF16, name="hd_bf", align_bytes=64)
+        ht_c = keep.tile([P, 2 * Q], U32, name="ht_c", align_bytes=64)
+        ht_s = keep.tile([P, 2 * Q], U8, name="ht_s", align_bytes=64)
+        hd_c = keep.tile([P, Q], U32, name="hd_c", align_bytes=64)
+        hd_s = keep.tile([P, Q], U8, name="hd_s", align_bytes=64)
+        l1_sb = keep.tile([P, 1], F32, name="l1_sb")
+        l2_sb = keep.tile([P, 1], F32, name="l2_sb")
+        nl1 = keep.tile([P, 1], F32, name="nl1")
+        nl2 = keep.tile([P, 1], F32, name="nl2")
+        warm_in = keep.tile([P, 1], F32, name="warm_in")
+        warm_out = keep.tile([P, 1], F32, name="warm_out")
+        ea = keep.tile([P, I], F32, name="ea", align_bytes=64)
+        eb = [keep.tile([P, HALF], F32, name=f"eb{h}", align_bytes=64) for h in range(2)]
+        dd = [keep.tile([P, HALF], F32, name=f"dd{h}", align_bytes=64) for h in range(2)]
+        pp = [keep.tile([P, HALF], F32, name=f"pp{h}", align_bytes=64) for h in range(2)]
+        yy = [keep.tile([P, HALF], F32, name=f"yy{h}", align_bytes=64) for h in range(2)]
+        ss = [keep.tile([P, 1], F32, name=f"ss{h}") for h in range(2)]
+        rr = keep.tile([P, 1], F32, name="rr")
+        a_ps = psum.tile([P, I], F32, name="a_ps")
+        b_ps = [psum.tile([P, HALF], F32, name=f"b_ps{h}") for h in range(2)]
+
+        nc.vector.memset(ets_win[:].bitcast(I32), 0)
+        nc.vector.memset(warm_in[:], 0.0)
+        nc.vector.memset(eds_win[:].bitcast(I32), 0)
+        nc.vector.memset(ets_1[:].bitcast(I32), 0)
+
+        nc.sync.dma_start(out=et_win[0][:].bitcast(I32), in_=et_words[0].bitcast(I32))
+        nc.sync.dma_start(offsets[:], offs)
+        ets_src = et_scales.bitcast(I32).rearrange("z (q r) c -> r q z c", r=4)
+        for r in range(4):
+            nc.scalar.dma_start(out=ets_win[r:P:SHIFT, :].bitcast(I32), in_=ets_src[r])
+        nc.scalar.activation(warm_out[:], warm_in[:], ACT.Exp)
+        nc.gpsimd.dma_start(out=l1_sb[:], in_=l1)
+        nc.gpsimd.dma_start(out=l2_sb[:], in_=l2)
+        nc.gpsimd.tensor_scalar(nl1[:], l1_sb[:], -1.0, 0.0, ALU.mult, ALU.add)
+        nc.gpsimd.tensor_scalar(nl2[:], l2_sb[:], -1.0, 0.0, ALU.mult, ALU.add)
+        nc.sync.dma_start(
+            out=ht_raw[:].rearrange("p z j q -> p z (j q)"),
+            in_=ht.rearrange("(z p j) q -> p z (j q)", z=2, j=PACK),
+        )
+        nc.sync.dma_start(out=et_win[1][:].bitcast(I32), in_=et_words[1].bitcast(I32))
+        nc.sync.dma_start(
+            out=hd_raw[:].rearrange("p j q -> p (j q)"),
+            in_=hd.rearrange("(p j) q -> p (j q)", j=PACK),
+        )
+        nc.sync.dma_start(out=ed_win[:].bitcast(I32), in_=ed_words[0].rearrange("p n t -> p (n t)").bitcast(I32))
+        eds_src = ed_scales[0].bitcast(I32)
+        for q in range(4):
+            row = 32 * q + ED_ROW
+            nc.scalar.dma_start(out=eds_win[row : row + 4, :].bitcast(I32), in_=eds_src[4 * q : 4 * q + 4, :])
+
+        nc.vector.tensor_copy(ets_g[:], ets_win[:].indirect(offsets[:]))
+        nc.scalar.dma_start(out=ets_1[0 : P - SHIFT, :].bitcast(I32), in_=ets_g[SHIFT:P, :].bitcast(I32))
+        nc.vector.tensor_copy(et_g[0][:], et_win[0][:].indirect(offsets[:]))
+        for z in range(2):
+            nc.scalar.copy(out=ht_bf[:, z], in_=ht_raw[:, z].rearrange("p j q -> p q j"))
+        nc.vector.tensor_copy(et_g[1][:], et_win[1][:].indirect(offsets[:]))
+        nc.vector.quantize_mx(
+            out=ht_c[:].bitcast(FP8X4), scales=ht_s[:], in_=ht_bf[:].rearrange("p z q j -> p (z q j)")
+        )
+        nc.scalar.copy(out=hd_bf[:], in_=hd_raw[:].rearrange("p j q -> p q j"))
+        nc.vector.tensor_copy(eds_g[:], eds_win[:].indirect(offsets[:]))
+        planes = (ets_g, ets_1)
+        for z in range(2):
+            cols = slice(z * Q, (z + 1) * Q)
+            nc.tensor.matmul_mx(
+                out=a_ps[:],
+                lhsT=ht_c[:, cols].bitcast(FP8X4),
+                lhsT_scale=ht_s[:, cols],
+                rhs=et_g[z][:].bitcast(FP4X4),
+                rhs_scale=planes[z][:],
+                start=(z == 0),
+                stop=(z == 1),
+            )
+        nc.vector.quantize_mx(out=hd_c[:].bitcast(FP8X4), scales=hd_s[:], in_=hd_bf[:].rearrange("p q j -> p (q j)"))
+        nc.scalar.activation(ea[:], a_ps[:], ACT.Exp, bias=nl1[:])
+
+        for h in range(2):
+            cols = slice(h * HALF, (h + 1) * HALF)
+            nc.vector.tensor_copy(ed_g[h][:], ed_win[:].indirect(offsets[:, h * HALF // 16 : (h + 1) * HALF // 16]))
+            nc.tensor.matmul_mx(
+                out=b_ps[h][:],
+                lhsT=hd_c[:].bitcast(FP8X4),
+                lhsT_scale=hd_s[:],
+                rhs=ed_g[h][:].bitcast(FP8X4),
+                rhs_scale=eds_g[ED_ROW:P, cols],
+                start=True,
+                stop=True,
+            )
+            nc.scalar.activation(eb[h][:], b_ps[h][:], ACT.Exp, bias=nl2[:])
+        for h in range(2):
+            cols = slice(h * HALF, (h + 1) * HALF)
+            nc.vector.tensor_tensor(dd[h][:], ea[:, cols], eb[h][:], ALU.subtract)
+            nc.vector.tensor_scalar(
+                pp[h][:], dd[h][:], 0.0, (None if h == 0 else ss[0][:]), ALU.max, ALU.add, accum_out=ss[h][:]
+            )
+        nc.vector.reciprocal(rr[:], ss[1][:])
+        for h, queue in enumerate((nc.sync, nc.scalar)):
+            cols = slice(h * HALF, (h + 1) * HALF)
+            nc.vector.tensor_scalar(yy[h][:], pp[h][:], rr[:], float(I), ALU.mult, ALU.mult)
+            queue.dma_start(out=out[:, cols], in_=yy[h][:])

@@ -37,9 +37,8 @@ def tile_attend_speculate_residual_kernel(tc, ht, hd, et_words, et_scales, ed_wo
         et_g = [keep.tile([P, I], U16, name=f"et_g{z}", align_bytes=64) for z in range(2)]
         ed_g = [keep.tile([P, HALF], U32, name=f"ed_g{h}", align_bytes=64) for h in range(2)]
         ets_g = keep.tile([P, I], U8, name="ets_g", align_bytes=64)
-        ets_1 = keep.tile([P, I], U8, name="ets_1", align_bytes=64)
         eds_g = keep.tile([P, I], U8, name="eds_g", align_bytes=64)
-        ht_raw = keep.tile([P, 2, PACK, Q], F32, name="ht_raw", align_bytes=64)
+        ht_raw = keep.tile([P, 2, PACK, Q], F32, name="ht_raw", tag="ht_raw", align_bytes=64)
         hd_raw = keep.tile([P, PACK, Q], F32, name="hd_raw", align_bytes=64)
         ht_bf = keep.tile([P, 2, Q, PACK], BF16, name="ht_bf", align_bytes=64)
         hd_bf = keep.tile([P, Q, PACK], BF16, name="hd_bf", align_bytes=64)
@@ -66,13 +65,12 @@ def tile_attend_speculate_residual_kernel(tc, ht, hd, et_words, et_scales, ed_wo
         nc.vector.memset(ets_win[:].bitcast(I32), 0)
         nc.vector.memset(warm_in[:], 0.0)
         nc.vector.memset(eds_win[:].bitcast(I32), 0)
-        nc.vector.memset(ets_1[:].bitcast(I32), 0)
 
-        nc.sync.dma_start(out=et_win[0][:].bitcast(I32), in_=et_words[0].bitcast(I32))
         nc.sync.dma_start(offsets[:], offs)
+        nc.sync.dma_start(out=et_win[0][:].bitcast(I32), in_=et_words[0].bitcast(I32))
         ets_src = et_scales.bitcast(I32).rearrange("z (q r) c -> r q z c", r=4)
         for r in range(4):
-            nc.scalar.dma_start(out=ets_win[r:P:SHIFT, :].bitcast(I32), in_=ets_src[r])
+            nc.sync.dma_start(out=ets_win[r:P:SHIFT, :].bitcast(I32), in_=ets_src[r])
         nc.scalar.activation(warm_out[:], warm_in[:], ACT.Exp)
         nc.gpsimd.dma_start(out=l1_sb[:], in_=l1)
         nc.gpsimd.dma_start(out=l2_sb[:], in_=l2)
@@ -87,17 +85,17 @@ def tile_attend_speculate_residual_kernel(tc, ht, hd, et_words, et_scales, ed_wo
             out=hd_raw[:].rearrange("p j q -> p (j q)"),
             in_=hd.rearrange("(p j) q -> p (j q)", j=PACK),
         )
-        nc.sync.dma_start(out=ed_win[:].bitcast(I32), in_=ed_words[0].rearrange("p n t -> p (n t)").bitcast(I32))
         eds_src = ed_scales[0].bitcast(I32)
         for q in range(4):
             row = 32 * q + ED_ROW
-            nc.scalar.dma_start(out=eds_win[row : row + 4, :].bitcast(I32), in_=eds_src[4 * q : 4 * q + 4, :])
-
+            nc.sync.dma_start(out=eds_win[row : row + 4, :].bitcast(I32), in_=eds_src[4 * q : 4 * q + 4, :])
+        nc.sync.dma_start(out=ed_win[:].bitcast(I32), in_=ed_words[0].rearrange("p n t -> p (n t)").bitcast(I32))
         nc.vector.tensor_copy(ets_g[:], ets_win[:].indirect(offsets[:]))
-        nc.scalar.dma_start(out=ets_1[0 : P - SHIFT, :].bitcast(I32), in_=ets_g[SHIFT:P, :].bitcast(I32))
         nc.vector.tensor_copy(et_g[0][:], et_win[0][:].indirect(offsets[:]))
         for z in range(2):
             nc.scalar.copy(out=ht_bf[:, z], in_=ht_raw[:, z].rearrange("p j q -> p q j"))
+        ets_1 = keep.tile([P, I], U8, name="ets_1", tag="ht_raw", align_bytes=64)
+        nc.scalar.dma_start(out=ets_1[0 : P - SHIFT, :].bitcast(I32), in_=ets_g[SHIFT:P, :].bitcast(I32))
         nc.vector.tensor_copy(et_g[1][:], et_win[1][:].indirect(offsets[:]))
         nc.vector.quantize_mx(
             out=ht_c[:].bitcast(FP8X4), scales=ht_s[:], in_=ht_bf[:].rearrange("p z q j -> p (z q j)")

@@ -39,7 +39,7 @@ def tile_attend_speculate_residual_kernel(tc, ht, hd, et_words, et_scales, ed_wo
         ets_g = keep.tile([P, I], U8, name="ets_g", align_bytes=64)
         eds_g = keep.tile([P, I], U8, name="eds_g", align_bytes=64)
         ht_raw = keep.tile([P, 2, PACK, Q], F32, name="ht_raw", tag="ht_raw", align_bytes=64)
-        hd_raw = keep.tile([P, PACK, Q], F32, name="hd_raw", align_bytes=64)
+        hd_raw = keep.tile([P, PACK, Q], F32, name="hd_raw", tag="hd_raw", align_bytes=64)
         ht_bf = keep.tile([P, 2, Q, PACK], BF16, name="ht_bf", align_bytes=64)
         hd_bf = keep.tile([P, Q, PACK], BF16, name="hd_bf", align_bytes=64)
         ht_c = keep.tile([P, 2 * Q], U32, name="ht_c", align_bytes=64)
@@ -48,8 +48,6 @@ def tile_attend_speculate_residual_kernel(tc, ht, hd, et_words, et_scales, ed_wo
         hd_s = keep.tile([P, Q], U8, name="hd_s", align_bytes=64)
         l1_sb = keep.tile([P, 1], F32, name="l1_sb")
         l2_sb = keep.tile([P, 1], F32, name="l2_sb")
-        nl1 = keep.tile([P, 1], F32, name="nl1")
-        nl2 = keep.tile([P, 1], F32, name="nl2")
         warm_in = keep.tile([P, 1], F32, name="warm_in")
         warm_out = keep.tile([P, 1], F32, name="warm_out")
         ea = keep.tile([P, I], F32, name="ea", align_bytes=64)
@@ -74,8 +72,6 @@ def tile_attend_speculate_residual_kernel(tc, ht, hd, et_words, et_scales, ed_wo
         nc.scalar.activation(warm_out[:], warm_in[:], ACT.Exp)
         nc.gpsimd.dma_start(out=l1_sb[:], in_=l1)
         nc.gpsimd.dma_start(out=l2_sb[:], in_=l2)
-        nc.gpsimd.tensor_scalar(nl1[:], l1_sb[:], -1.0, 0.0, ALU.mult, ALU.add)
-        nc.gpsimd.tensor_scalar(nl2[:], l2_sb[:], -1.0, 0.0, ALU.mult, ALU.add)
         nc.sync.dma_start(
             out=ht_raw[:].rearrange("p z j q -> p z (j q)"),
             in_=ht.rearrange("(z p j) q -> p z (j q)", z=2, j=PACK),
@@ -101,6 +97,9 @@ def tile_attend_speculate_residual_kernel(tc, ht, hd, et_words, et_scales, ed_wo
             out=ht_c[:].bitcast(FP8X4), scales=ht_s[:], in_=ht_bf[:].rearrange("p z q j -> p (z q j)")
         )
         nc.scalar.copy(out=hd_bf[:], in_=hd_raw[:].rearrange("p j q -> p q j"))
+        nl = keep.tile([P, 2], F32, name="nl", tag="hd_raw", align_bytes=64)
+        nc.scalar.mul(nl[:, 0:1], l1_sb[:], -1.0)
+        nc.scalar.mul(nl[:, 1:2], l2_sb[:], -1.0)
         nc.vector.tensor_copy(eds_g[:], eds_win[:].indirect(offsets[:]))
         planes = (ets_g, ets_1)
         for z in range(2):
@@ -115,7 +114,7 @@ def tile_attend_speculate_residual_kernel(tc, ht, hd, et_words, et_scales, ed_wo
                 stop=(z == 1),
             )
         nc.vector.quantize_mx(out=hd_c[:].bitcast(FP8X4), scales=hd_s[:], in_=hd_bf[:].rearrange("p q j -> p (q j)"))
-        nc.scalar.activation(ea[:], a_ps[:], ACT.Exp, bias=nl1[:])
+        nc.scalar.activation(ea[:], a_ps[:], ACT.Exp, bias=nl[:, 0:1])
 
         for h in range(2):
             cols = slice(h * HALF, (h + 1) * HALF)
@@ -129,13 +128,12 @@ def tile_attend_speculate_residual_kernel(tc, ht, hd, et_words, et_scales, ed_wo
                 start=True,
                 stop=True,
             )
-            nc.scalar.activation(eb[h][:], b_ps[h][:], ACT.Exp, bias=nl2[:])
+            nc.scalar.activation(eb[h][:], b_ps[h][:], ACT.Exp, bias=nl[:, 1:2])
         for h in range(2):
             cols = slice(h * HALF, (h + 1) * HALF)
             nc.vector.tensor_tensor(dd[h][:], ea[:, cols], eb[h][:], ALU.subtract)
-            nc.vector.tensor_scalar(
-                pp[h][:], dd[h][:], 0.0, (None if h == 0 else ss[0][:]), ALU.max, ALU.add, accum_out=ss[h][:]
-            )
+        nc.scalar.activation(pp[0][:], dd[0][:], ACT.Relu, accum_out=ss[0][:])
+        nc.vector.tensor_scalar(pp[1][:], dd[1][:], 0.0, ss[0][:], ALU.max, ALU.add, accum_out=ss[1][:])
         nc.vector.reciprocal(rr[:], ss[1][:])
         for h, queue in enumerate((nc.sync, nc.scalar)):
             cols = slice(h * HALF, (h + 1) * HALF)

@@ -51,21 +51,22 @@ def tile_attend_speculate_residual_kernel(tc, ht, hd, et_words, et_scales, ed_wo
         warm_in = keep.tile([P, 1], F32, name="warm_in")
         warm_out = keep.tile([P, 1], F32, name="warm_out")
         ea = keep.tile([P, I], F32, name="ea", align_bytes=64)
-        eb = [keep.tile([P, HALF], F32, name=f"eb{h}", align_bytes=64) for h in range(2)]
-        dd = [keep.tile([P, HALF], F32, name=f"dd{h}", align_bytes=64) for h in range(2)]
-        pp = [keep.tile([P, HALF], F32, name=f"pp{h}", align_bytes=64) for h in range(2)]
+        eb = keep.tile([P, I], F32, name="eb", align_bytes=64)
+        dd = keep.tile([P, I], F32, name="dd", align_bytes=64)
+        pp = keep.tile([P, I], F32, name="pp", align_bytes=64)
         yy = [keep.tile([P, HALF], F32, name=f"yy{h}", align_bytes=64) for h in range(2)]
-        ss = [keep.tile([P, 1], F32, name=f"ss{h}") for h in range(2)]
+        ss = keep.tile([P, 1], F32, name="ss")
         rr = keep.tile([P, 1], F32, name="rr")
         a_ps = psum.tile([P, I], F32, name="a_ps")
-        b_ps = [psum.tile([P, HALF], F32, name=f"b_ps{h}") for h in range(2)]
+        pieces = [(h, lo, lo + HALF // 2) for h in range(2) for lo in (0, HALF // 2)]
+        b_ps = [psum.tile([P, hi - lo], F32, name=f"b_ps{n}") for n, (h, lo, hi) in enumerate(pieces)]
 
         nc.vector.memset(ets_win[:].bitcast(I32), 0)
         nc.vector.memset(warm_in[:], 0.0)
         nc.vector.memset(eds_win[:].bitcast(I32), 0)
 
-        nc.sync.dma_start(offsets[:], offs)
         nc.sync.dma_start(out=et_win[0][:].bitcast(I32), in_=et_words[0].bitcast(I32))
+        nc.sync.dma_start(offsets[:], offs)
         ets_src = et_scales.bitcast(I32).rearrange("z (q r) c -> r q z c", r=4)
         for r in range(4):
             nc.sync.dma_start(out=ets_win[r:P:SHIFT, :].bitcast(I32), in_=ets_src[r])
@@ -117,25 +118,23 @@ def tile_attend_speculate_residual_kernel(tc, ht, hd, et_words, et_scales, ed_wo
         nc.scalar.activation(ea[:], a_ps[:], ACT.Exp, bias=nl[:, 0:1])
 
         for h in range(2):
-            cols = slice(h * HALF, (h + 1) * HALF)
             nc.vector.tensor_copy(ed_g[h][:], ed_win[:].indirect(offsets[:, h * HALF // 16 : (h + 1) * HALF // 16]))
+        for n, (h, lo, hi) in enumerate(pieces):
+            cols = slice(h * HALF + lo, h * HALF + hi)
             nc.tensor.matmul_mx(
-                out=b_ps[h][:],
+                out=b_ps[n][:],
                 lhsT=hd_c[:].bitcast(FP8X4),
                 lhsT_scale=hd_s[:],
-                rhs=ed_g[h][:].bitcast(FP8X4),
+                rhs=ed_g[h][:, lo:hi].bitcast(FP8X4),
                 rhs_scale=eds_g[ED_ROW:P, cols],
                 start=True,
                 stop=True,
             )
-            nc.scalar.activation(eb[h][:], b_ps[h][:], ACT.Exp, bias=nl[:, 1:2])
-        for h in range(2):
-            cols = slice(h * HALF, (h + 1) * HALF)
-            nc.vector.tensor_tensor(dd[h][:], ea[:, cols], eb[h][:], ALU.subtract)
-        nc.scalar.activation(pp[0][:], dd[0][:], ACT.Relu, accum_out=ss[0][:])
-        nc.vector.tensor_scalar(pp[1][:], dd[1][:], 0.0, ss[0][:], ALU.max, ALU.add, accum_out=ss[1][:])
-        nc.vector.reciprocal(rr[:], ss[1][:])
-        for h, queue in enumerate((nc.sync, nc.scalar)):
-            cols = slice(h * HALF, (h + 1) * HALF)
-            nc.vector.tensor_scalar(yy[h][:], pp[h][:], rr[:], float(I), ALU.mult, ALU.mult)
-            queue.dma_start(out=out[:, cols], in_=yy[h][:])
+            nc.scalar.activation(eb[:, cols], b_ps[n][:], ACT.Exp, bias=nl[:, 1:2])
+            nc.vector.tensor_tensor(dd[:, cols], ea[:, cols], eb[:, cols], ALU.subtract)
+        nc.scalar.activation(pp[:], dd[:], ACT.Relu, scale=1.0 / I, accum_out=ss[:])
+        nc.vector.reciprocal(rr[:], ss[:])
+        nc.vector.tensor_scalar(yy[0][:], dd[:, :HALF], 0.0, rr[:], ALU.max, ALU.mult)
+        nc.sync.dma_start(out=out[:, :HALF], in_=yy[0][:])
+        nc.scalar.activation(yy[1][:], dd[:, HALF:], ACT.Relu, scale=rr[:])
+        nc.scalar.dma_start(out=out[:, HALF:], in_=yy[1][:])

@@ -82,10 +82,9 @@ def tile_attend_speculate_residual_kernel(tc, ht, hd, et_words, et_scales, ed_wo
             out=hd_raw[:].rearrange("p j q -> p (j q)"),
             in_=hd.rearrange("(p j) q -> p (j q)", j=PACK),
         )
-        eds_src = ed_scales[0].bitcast(I32)
-        for q in range(4):
-            row = 32 * q + ED_ROW
-            nc.sync.dma_start(out=eds_win[row : row + 4, :].bitcast(I32), in_=eds_src[4 * q : 4 * q + 4, :])
+        eds_src = ed_scales[0].bitcast(I32).rearrange("(q r) c -> r q c", r=4)
+        for r in range(4):
+            nc.sync.dma_start(out=eds_win[ED_ROW + r : P : 32, :].bitcast(I32), in_=eds_src[r])
         nc.sync.dma_start(out=ed_win[:].bitcast(I32), in_=ed_words[0].rearrange("p n t -> p (n t)").bitcast(I32))
         nc.vector.tensor_copy(ets_g[:], ets_win[:].indirect(offsets[:]))
         nc.vector.tensor_copy(et_g[0][:], et_win[0][:].indirect(offsets[:]))

@@ -78,13 +78,13 @@ def tile_attend_speculate_residual_kernel(tc, ht, hd, et_words, et_scales, ed_wo
             in_=ht.rearrange("(z p j) q -> p z (j q)", z=2, j=PACK),
         )
         nc.sync.dma_start(out=et_win[1][:].bitcast(I32), in_=et_words[1].bitcast(I32))
+        eds_src = ed_scales[0].bitcast(I32).rearrange("(q r) c -> r q c", r=4)
+        for r in range(4):
+            nc.sync.dma_start(out=eds_win[ED_ROW + r : P : 32, :].bitcast(I32), in_=eds_src[r])
         nc.sync.dma_start(
             out=hd_raw[:].rearrange("p j q -> p (j q)"),
             in_=hd.rearrange("(p j) q -> p (j q)", j=PACK),
         )
-        eds_src = ed_scales[0].bitcast(I32).rearrange("(q r) c -> r q c", r=4)
-        for r in range(4):
-            nc.sync.dma_start(out=eds_win[ED_ROW + r : P : 32, :].bitcast(I32), in_=eds_src[r])
         nc.sync.dma_start(out=ed_win[:].bitcast(I32), in_=ed_words[0].rearrange("p n t -> p (n t)").bitcast(I32))
         nc.vector.tensor_copy(ets_g[:], ets_win[:].indirect(offsets[:]))
         nc.vector.tensor_copy(et_g[0][:], et_win[0][:].indirect(offsets[:]))

@@ -19,8 +19,6 @@ ACT = mybir.ActivationFunctionType
 P = 128
 PACK = 4
 HALF = I // 2
-SHIFT = 16
-ED_ROW = 4
 
 
 def tile_attend_speculate_residual_kernel(tc, ht, hd, et_words, et_scales, ed_words, ed_scales, l1, l2, offs, out):
@@ -61,37 +59,44 @@ def tile_attend_speculate_residual_kernel(tc, ht, hd, et_words, et_scales, ed_wo
         pieces = [(h, lo, lo + HALF // 2) for h in range(2) for lo in (0, HALF // 2)]
         b_ps = [psum.tile([P, hi - lo], F32, name=f"b_ps{n}") for n, (h, lo, hi) in enumerate(pieces)]
 
-        nc.vector.memset(ets_win[:].bitcast(I32), 0)
-        nc.vector.memset(warm_in[:], 0.0)
         nc.vector.memset(eds_win[:].bitcast(I32), 0)
+        nc.vector.memset(warm_in[:], 0.0)
+        nc.vector.memset(ets_win[32:64, :].bitcast(I32), 0)
+        nc.vector.memset(ets_win[64:P, :].bitcast(I32), 0)
 
-        nc.sync.dma_start(out=et_win[0][:].bitcast(I32), in_=et_words[0].bitcast(I32))
+        nc.sync.dma_start(out=ets_win[0:32, :].bitcast(I32), in_=et_scales.bitcast(I32).rearrange("z f c -> (z f) c"))
         nc.sync.dma_start(offsets[:], offs)
-        ets_src = et_scales.bitcast(I32).rearrange("z (q r) c -> r q z c", r=4)
-        for r in range(4):
-            nc.sync.dma_start(out=ets_win[r:P:SHIFT, :].bitcast(I32), in_=ets_src[r])
+        nc.sync.dma_start(out=et_win[0][:].bitcast(I32), in_=et_words[0].bitcast(I32))
+        nc.sync.dma_start(out=eds_win[0:P:8, :].bitcast(I32), in_=ed_scales[0].bitcast(I32))
         nc.scalar.activation(warm_out[:], warm_in[:], ACT.Exp)
-        nc.gpsimd.dma_start(out=l1_sb[:], in_=l1)
+        nc.sync.dma_start(out=l1_sb[:], in_=l1)
         nc.gpsimd.dma_start(out=l2_sb[:], in_=l2)
         nc.sync.dma_start(
             out=ht_raw[:].rearrange("p z j q -> p z (j q)"),
             in_=ht.rearrange("(z p j) q -> p z (j q)", z=2, j=PACK),
         )
         nc.sync.dma_start(out=et_win[1][:].bitcast(I32), in_=et_words[1].bitcast(I32))
-        eds_src = ed_scales[0].bitcast(I32).rearrange("(q r) c -> r q c", r=4)
-        for r in range(4):
-            nc.sync.dma_start(out=eds_win[ED_ROW + r : P : 32, :].bitcast(I32), in_=eds_src[r])
         nc.sync.dma_start(
             out=hd_raw[:].rearrange("p j q -> p (j q)"),
             in_=hd.rearrange("(p j) q -> p (j q)", j=PACK),
         )
         nc.sync.dma_start(out=ed_win[:].bitcast(I32), in_=ed_words[0].rearrange("p n t -> p (n t)").bitcast(I32))
         nc.vector.tensor_copy(ets_g[:], ets_win[:].indirect(offsets[:]))
+        ets_0 = keep.tile([P, I], U8, name="ets_0", align_bytes=64)
+        for q in range(4):
+            nc.scalar.dma_start(out=ets_0[32 * q : 32 * q + 4, :].bitcast(I32), in_=ets_g[4 * q : 4 * q + 4, :].bitcast(I32))
         nc.vector.tensor_copy(et_g[0][:], et_win[0][:].indirect(offsets[:]))
         for z in range(2):
             nc.scalar.copy(out=ht_bf[:, z], in_=ht_raw[:, z].rearrange("p j q -> p q j"))
-        ets_1 = keep.tile([P, I], U8, name="ets_1", tag="ht_raw", align_bytes=64)
-        nc.scalar.dma_start(out=ets_1[0 : P - SHIFT, :].bitcast(I32), in_=ets_g[SHIFT:P, :].bitcast(I32))
+        late = keep.tile([P, 2 * I], U8, name="late", tag="ht_raw", align_bytes=64)
+        ets_1 = late[:, :I]
+        for q in range(4):
+            nc.scalar.dma_start(
+                out=late[32 * q : 32 * q + 4, :I].bitcast(I32), in_=ets_g[16 + 4 * q : 20 + 4 * q, :].bitcast(I32)
+            )
+        nc.vector.tensor_copy(eds_g[:], eds_win[:].indirect(offsets[:]))
+        for r, queue in enumerate((nc.gpsimd, nc.scalar, nc.scalar, nc.scalar)):
+            queue.dma_start(out=late[r:P:32, I:].bitcast(I32), in_=eds_g[8 * r : P : 32, :].bitcast(I32))
         nc.vector.tensor_copy(et_g[1][:], et_win[1][:].indirect(offsets[:]))
         nc.vector.quantize_mx(
             out=ht_c[:].bitcast(FP8X4), scales=ht_s[:], in_=ht_bf[:].rearrange("p z q j -> p (z q j)")
@@ -100,8 +105,7 @@ def tile_attend_speculate_residual_kernel(tc, ht, hd, et_words, et_scales, ed_wo
         nl = keep.tile([P, 2], F32, name="nl", tag="hd_raw", align_bytes=64)
         nc.scalar.mul(nl[:, 0:1], l1_sb[:], -1.0)
         nc.scalar.mul(nl[:, 1:2], l2_sb[:], -1.0)
-        nc.vector.tensor_copy(eds_g[:], eds_win[:].indirect(offsets[:]))
-        planes = (ets_g, ets_1)
+        planes = (ets_0[:], ets_1)
         for z in range(2):
             cols = slice(z * Q, (z + 1) * Q)
             nc.tensor.matmul_mx(
@@ -109,7 +113,7 @@ def tile_attend_speculate_residual_kernel(tc, ht, hd, et_words, et_scales, ed_wo
                 lhsT=ht_c[:, cols].bitcast(FP8X4),
                 lhsT_scale=ht_s[:, cols],
                 rhs=et_g[z][:].bitcast(FP4X4),
-                rhs_scale=planes[z][:],
+                rhs_scale=planes[z],
                 start=(z == 0),
                 stop=(z == 1),
             )
@@ -125,7 +129,7 @@ def tile_attend_speculate_residual_kernel(tc, ht, hd, et_words, et_scales, ed_wo
                 lhsT=hd_c[:].bitcast(FP8X4),
                 lhsT_scale=hd_s[:],
                 rhs=ed_g[h][:, lo:hi].bitcast(FP8X4),
-                rhs_scale=eds_g[ED_ROW:P, cols],
+                rhs_scale=late[:, I + cols.start : I + cols.stop],
                 start=True,
                 stop=True,
             )

@@ -69,7 +69,7 @@ def tile_attend_speculate_residual_kernel(tc, ht, hd, et_words, et_scales, ed_wo
         nc.sync.dma_start(out=et_win[0][:].bitcast(I32), in_=et_words[0].bitcast(I32))
         nc.sync.dma_start(out=eds_win[0:P:8, :].bitcast(I32), in_=ed_scales[0].bitcast(I32))
         nc.scalar.activation(warm_out[:], warm_in[:], ACT.Exp)
-        nc.sync.dma_start(out=l1_sb[:], in_=l1)
+        nc.gpsimd.dma_start(out=l1_sb[:], in_=l1)
         nc.gpsimd.dma_start(out=l2_sb[:], in_=l2)
         nc.sync.dma_start(
             out=ht_raw[:].rearrange("p z j q -> p z (j q)"),
@@ -85,18 +85,23 @@ def tile_attend_speculate_residual_kernel(tc, ht, hd, et_words, et_scales, ed_wo
         ets_0 = keep.tile([P, I], U8, name="ets_0", align_bytes=64)
         for q in range(4):
             nc.scalar.dma_start(out=ets_0[32 * q : 32 * q + 4, :].bitcast(I32), in_=ets_g[4 * q : 4 * q + 4, :].bitcast(I32))
+        ets_1 = keep.tile([P, I], U8, name="ets_1", align_bytes=64)
+
+        def move_pass_1(q, queue):
+            queue.dma_start(
+                out=ets_1[32 * q : 32 * q + 4, :].bitcast(I32), in_=ets_g[16 + 4 * q : 20 + 4 * q, :].bitcast(I32)
+            )
+
+        for q, queue in enumerate((nc.gpsimd, nc.gpsimd, nc.scalar)):
+            move_pass_1(q, queue)
         nc.vector.tensor_copy(et_g[0][:], et_win[0][:].indirect(offsets[:]))
         for z in range(2):
             nc.scalar.copy(out=ht_bf[:, z], in_=ht_raw[:, z].rearrange("p j q -> p q j"))
-        late = keep.tile([P, 2 * I], U8, name="late", tag="ht_raw", align_bytes=64)
-        ets_1 = late[:, :I]
-        for q in range(4):
-            nc.scalar.dma_start(
-                out=late[32 * q : 32 * q + 4, :I].bitcast(I32), in_=ets_g[16 + 4 * q : 20 + 4 * q, :].bitcast(I32)
-            )
+        move_pass_1(3, nc.scalar)
         nc.vector.tensor_copy(eds_g[:], eds_win[:].indirect(offsets[:]))
-        for r, queue in enumerate((nc.gpsimd, nc.scalar, nc.scalar, nc.scalar)):
-            queue.dma_start(out=late[r:P:32, I:].bitcast(I32), in_=eds_g[8 * r : P : 32, :].bitcast(I32))
+        eds_p = keep.tile([P, I], U8, name="eds_p", align_bytes=64)
+        for r in range(4):
+            nc.sync.dma_start(out=eds_p[r:P:32, :].bitcast(I32), in_=eds_g[8 * r : P : 32, :].bitcast(I32))
         nc.vector.tensor_copy(et_g[1][:], et_win[1][:].indirect(offsets[:]))
         nc.vector.quantize_mx(
             out=ht_c[:].bitcast(FP8X4), scales=ht_s[:], in_=ht_bf[:].rearrange("p z q j -> p (z q j)")
@@ -105,7 +110,7 @@ def tile_attend_speculate_residual_kernel(tc, ht, hd, et_words, et_scales, ed_wo
         nl = keep.tile([P, 2], F32, name="nl", tag="hd_raw", align_bytes=64)
         nc.scalar.mul(nl[:, 0:1], l1_sb[:], -1.0)
         nc.scalar.mul(nl[:, 1:2], l2_sb[:], -1.0)
-        planes = (ets_0[:], ets_1)
+        planes = (ets_0[:], ets_1[:])
         for z in range(2):
             cols = slice(z * Q, (z + 1) * Q)
             nc.tensor.matmul_mx(
@@ -129,7 +134,7 @@ def tile_attend_speculate_residual_kernel(tc, ht, hd, et_words, et_scales, ed_wo
                 lhsT=hd_c[:].bitcast(FP8X4),
                 lhsT_scale=hd_s[:],
                 rhs=ed_g[h][:, lo:hi].bitcast(FP8X4),
-                rhs_scale=late[:, I + cols.start : I + cols.stop],
+                rhs_scale=eds_p[:, cols],
                 start=True,
                 stop=True,
             )

@@ -55,7 +55,7 @@ def tile_attend_speculate_residual_kernel(tc, ht, hd, et_words, et_scales, ed_wo
         yy = [keep.tile([P, HALF], F32, name=f"yy{h}", align_bytes=64) for h in range(2)]
         ss = keep.tile([P, 1], F32, name="ss")
         rr = keep.tile([P, 1], F32, name="rr")
-        a_ps = psum.tile([P, I], F32, name="a_ps")
+        a_ps = [psum.tile([P, Q], F32, name=f"a_ps{n}") for n in range(I // Q)]
         pieces = [(h, lo, lo + HALF // 2) for h in range(2) for lo in (0, HALF // 2)]
         b_ps = [psum.tile([P, hi - lo], F32, name=f"b_ps{n}") for n, (h, lo, hi) in enumerate(pieces)]
 
@@ -66,10 +66,10 @@ def tile_attend_speculate_residual_kernel(tc, ht, hd, et_words, et_scales, ed_wo
 
         nc.sync.dma_start(out=ets_win[0:32, :].bitcast(I32), in_=et_scales.bitcast(I32).rearrange("z f c -> (z f) c"))
         nc.sync.dma_start(offsets[:], offs)
-        nc.sync.dma_start(out=et_win[0][:].bitcast(I32), in_=et_words[0].bitcast(I32))
+        nc.scalar.dma_start(out=et_win[0][:].bitcast(I32), in_=et_words[0].bitcast(I32))
         nc.sync.dma_start(out=eds_win[0:P:8, :].bitcast(I32), in_=ed_scales[0].bitcast(I32))
         nc.scalar.activation(warm_out[:], warm_in[:], ACT.Exp)
-        nc.gpsimd.dma_start(out=l1_sb[:], in_=l1)
+        nc.sync.dma_start(out=l1_sb[:], in_=l1)
         nc.gpsimd.dma_start(out=l2_sb[:], in_=l2)
         nc.sync.dma_start(
             out=ht_raw[:].rearrange("p z j q -> p z (j q)"),
@@ -110,20 +110,23 @@ def tile_attend_speculate_residual_kernel(tc, ht, hd, et_words, et_scales, ed_wo
         nl = keep.tile([P, 2], F32, name="nl", tag="hd_raw", align_bytes=64)
         nc.scalar.mul(nl[:, 0:1], l1_sb[:], -1.0)
         nc.scalar.mul(nl[:, 1:2], l2_sb[:], -1.0)
-        planes = (ets_0[:], ets_1[:])
+        planes = (ets_0, ets_1)
         for z in range(2):
-            cols = slice(z * Q, (z + 1) * Q)
-            nc.tensor.matmul_mx(
-                out=a_ps[:],
-                lhsT=ht_c[:, cols].bitcast(FP8X4),
-                lhsT_scale=ht_s[:, cols],
-                rhs=et_g[z][:].bitcast(FP4X4),
-                rhs_scale=planes[z],
-                start=(z == 0),
-                stop=(z == 1),
-            )
+            rows = slice(z * Q, (z + 1) * Q)
+            for n in range(I // Q):
+                cols = slice(n * Q, (n + 1) * Q)
+                nc.tensor.matmul_mx(
+                    out=a_ps[n][:],
+                    lhsT=ht_c[:, rows].bitcast(FP8X4),
+                    lhsT_scale=ht_s[:, rows],
+                    rhs=et_g[z][:, cols].bitcast(FP4X4),
+                    rhs_scale=planes[z][:, cols],
+                    start=(z == 0),
+                    stop=(z == 1),
+                )
         nc.vector.quantize_mx(out=hd_c[:].bitcast(FP8X4), scales=hd_s[:], in_=hd_bf[:].rearrange("p q j -> p (q j)"))
-        nc.scalar.activation(ea[:], a_ps[:], ACT.Exp, bias=nl[:, 0:1])
+        for n in range(I // Q):
+            nc.scalar.activation(ea[:, n * Q : (n + 1) * Q], a_ps[n][:], ACT.Exp, bias=nl[:, 0:1])
 
         for h in range(2):
             nc.vector.tensor_copy(ed_g[h][:], ed_win[:].indirect(offsets[:, h * HALF // 16 : (h + 1) * HALF // 16]))

@@ -1,3 +1,4 @@
+import math
 from contextlib import ExitStack
 
 import concourse.mybir as mybir
@@ -19,6 +20,7 @@ ACT = mybir.ActivationFunctionType
 P = 128
 PACK = 4
 HALF = I // 2
+PAD = 8
 
 
 def tile_attend_speculate_residual_kernel(tc, ht, hd, et_words, et_scales, ed_words, ed_scales, l1, l2, offs, out):
@@ -48,10 +50,11 @@ def tile_attend_speculate_residual_kernel(tc, ht, hd, et_words, et_scales, ed_wo
         l2_sb = keep.tile([P, 1], F32, name="l2_sb")
         warm_in = keep.tile([P, 1], F32, name="warm_in")
         warm_out = keep.tile([P, 1], F32, name="warm_out")
-        ea = keep.tile([P, I], F32, name="ea", align_bytes=64)
-        eb = keep.tile([P, I], F32, name="eb", align_bytes=64)
+        ea = keep.tile([P, I + 2 * PAD], F32, name="ea", align_bytes=64)
+        eb = keep.tile([P, I + 2 * PAD], F32, name="eb", align_bytes=64)
         dd = keep.tile([P, I], F32, name="dd", align_bytes=64)
-        pp = keep.tile([P, I], F32, name="pp", align_bytes=64)
+        low = [keep.tile([P, HALF + PAD], F32, name=f"low{h}", align_bytes=64) for h in range(2)]
+        ea_sum = keep.tile([P, I // Q], F32, name="ea_sum")
         yy = [keep.tile([P, HALF], F32, name=f"yy{h}", align_bytes=64) for h in range(2)]
         ss = keep.tile([P, 1], F32, name="ss")
         rr = keep.tile([P, 1], F32, name="rr")
@@ -63,8 +66,10 @@ def tile_attend_speculate_residual_kernel(tc, ht, hd, et_words, et_scales, ed_wo
         nc.vector.memset(warm_in[:], 0.0)
         nc.vector.memset(ets_win[32:64, :].bitcast(I32), 0)
         nc.vector.memset(ets_win[64:P, :].bitcast(I32), 0)
+        nc.vector.memset(eb[:, :PAD], 0.0)
+        nc.vector.memset(eb[:, PAD + I :], 0.0)
 
-        nc.sync.dma_start(out=ets_win[0:32, :].bitcast(I32), in_=et_scales.bitcast(I32).rearrange("z f c -> (z f) c"))
+        nc.sync.dma_start(out=ets_win[0:32, :].bitcast(I32), in_=et_scales.bitcast(I32).rearrange("z f c -> f z c"))
         nc.sync.dma_start(offsets[:], offs)
         nc.scalar.dma_start(out=et_win[0][:].bitcast(I32), in_=et_words[0].bitcast(I32))
         nc.sync.dma_start(out=eds_win[0:P:8, :].bitcast(I32), in_=ed_scales[0].bitcast(I32))
@@ -82,22 +87,12 @@ def tile_attend_speculate_residual_kernel(tc, ht, hd, et_words, et_scales, ed_wo
         )
         nc.sync.dma_start(out=ed_win[:].bitcast(I32), in_=ed_words[0].rearrange("p n t -> p (n t)").bitcast(I32))
         nc.vector.tensor_copy(ets_g[:], ets_win[:].indirect(offsets[:]))
-        ets_0 = keep.tile([P, I], U8, name="ets_0", align_bytes=64)
+        ets_p = keep.tile([P, 2 * I], U8, name="ets_p", align_bytes=64)
         for q in range(4):
-            nc.scalar.dma_start(out=ets_0[32 * q : 32 * q + 4, :].bitcast(I32), in_=ets_g[4 * q : 4 * q + 4, :].bitcast(I32))
-        ets_1 = keep.tile([P, I], U8, name="ets_1", align_bytes=64)
-
-        def move_pass_1(q, queue):
-            queue.dma_start(
-                out=ets_1[32 * q : 32 * q + 4, :].bitcast(I32), in_=ets_g[16 + 4 * q : 20 + 4 * q, :].bitcast(I32)
-            )
-
-        for q, queue in enumerate((nc.gpsimd, nc.gpsimd, nc.scalar)):
-            move_pass_1(q, queue)
+            nc.scalar.dma_start(out=ets_p[32 * q : 32 * q + 4, :].bitcast(I32), in_=ets_g[8 * q : 8 * q + 8, :].bitcast(I32))
         nc.vector.tensor_copy(et_g[0][:], et_win[0][:].indirect(offsets[:]))
         for z in range(2):
             nc.scalar.copy(out=ht_bf[:, z], in_=ht_raw[:, z].rearrange("p j q -> p q j"))
-        move_pass_1(3, nc.scalar)
         nc.vector.tensor_copy(eds_g[:], eds_win[:].indirect(offsets[:]))
         eds_p = keep.tile([P, I], U8, name="eds_p", align_bytes=64)
         for r in range(4):
@@ -108,9 +103,8 @@ def tile_attend_speculate_residual_kernel(tc, ht, hd, et_words, et_scales, ed_wo
         )
         nc.scalar.copy(out=hd_bf[:], in_=hd_raw[:].rearrange("p j q -> p q j"))
         nl = keep.tile([P, 2], F32, name="nl", tag="hd_raw", align_bytes=64)
-        nc.scalar.mul(nl[:, 0:1], l1_sb[:], -1.0)
+        nc.scalar.activation(nl[:, 0:1], l1_sb[:], ACT.Copy, scale=-1.0, bias=-math.log(I))
         nc.scalar.mul(nl[:, 1:2], l2_sb[:], -1.0)
-        planes = (ets_0, ets_1)
         for z in range(2):
             rows = slice(z * Q, (z + 1) * Q)
             for n in range(I // Q):
@@ -120,13 +114,16 @@ def tile_attend_speculate_residual_kernel(tc, ht, hd, et_words, et_scales, ed_wo
                     lhsT=ht_c[:, rows].bitcast(FP8X4),
                     lhsT_scale=ht_s[:, rows],
                     rhs=et_g[z][:, cols].bitcast(FP4X4),
-                    rhs_scale=planes[z][:, cols],
+                    rhs_scale=ets_p[:, z * I + n * Q : z * I + (n + 1) * Q],
                     start=(z == 0),
                     stop=(z == 1),
                 )
         nc.vector.quantize_mx(out=hd_c[:].bitcast(FP8X4), scales=hd_s[:], in_=hd_bf[:].rearrange("p q j -> p (q j)"))
         for n in range(I // Q):
-            nc.scalar.activation(ea[:, n * Q : (n + 1) * Q], a_ps[n][:], ACT.Exp, bias=nl[:, 0:1])
+            nc.scalar.activation(
+                ea[:, PAD + n * Q : PAD + (n + 1) * Q], a_ps[n][:], ACT.Exp, bias=nl[:, 0:1], accum_out=ea_sum[:, n : n + 1]
+            )
+        nc.scalar.mul(ea[:, PAD - I // Q : PAD], ea_sum[:], -1.0)
 
         for h in range(2):
             nc.vector.tensor_copy(ed_g[h][:], ed_win[:].indirect(offsets[:, h * HALF // 16 : (h + 1) * HALF // 16]))
@@ -141,11 +138,25 @@ def tile_attend_speculate_residual_kernel(tc, ht, hd, et_words, et_scales, ed_wo
                 start=True,
                 stop=True,
             )
-            nc.scalar.activation(eb[:, cols], b_ps[n][:], ACT.Exp, bias=nl[:, 1:2])
-            nc.vector.tensor_tensor(dd[:, cols], ea[:, cols], eb[:, cols], ALU.subtract)
-        nc.scalar.activation(pp[:], dd[:], ACT.Relu, scale=1.0 / I, accum_out=ss[:])
+            nc.scalar.activation(eb[:, PAD + cols.start : PAD + cols.stop], b_ps[n][:], ACT.Exp, bias=nl[:, 1:2])
+
+        def lesser_sum(h, cols, total):
+            nc.vector.scalar_tensor_tensor(
+                low[h][:, : cols.stop - cols.start], eb[:, cols], 1.0 / I, ea[:, cols], ALU.mult, ALU.min, accum_out=total
+            )
+
+        def difference(lo, hi):
+            nc.vector.scalar_tensor_tensor(
+                dd[:, lo:hi], ea[:, PAD + lo : PAD + hi], -float(I), eb[:, PAD + lo : PAD + hi], ALU.mult, ALU.add
+            )
+
+        lesser_sum(0, slice(PAD - I // Q, PAD + HALF), ea[:, PAD + I : PAD + I + 1])
+        difference(0, HALF)
+        difference(HALF, HALF + Q)
+        lesser_sum(1, slice(PAD + HALF, PAD + I + 1), ss[:])
+        difference(HALF + Q, I)
         nc.vector.reciprocal(rr[:], ss[:])
-        nc.vector.tensor_scalar(yy[0][:], dd[:, :HALF], 0.0, rr[:], ALU.max, ALU.mult)
-        nc.sync.dma_start(out=out[:, :HALF], in_=yy[0][:])
-        nc.scalar.activation(yy[1][:], dd[:, HALF:], ACT.Relu, scale=rr[:])
-        nc.scalar.dma_start(out=out[:, HALF:], in_=yy[1][:])
+        nc.scalar.activation(yy[0][:], dd[:, :HALF], ACT.Relu, scale=rr[:])
+        nc.scalar.dma_start(out=out[:, :HALF], in_=yy[0][:])
+        nc.vector.tensor_scalar(yy[1][:], dd[:, HALF:], rr[:], 0.0, ALU.mult, ALU.max)
+        nc.sync.dma_start(out=out[:, HALF:], in_=yy[1][:])

@@ -71,15 +71,15 @@ def tile_attend_speculate_residual_kernel(tc, ht, hd, et_words, et_scales, ed_wo
 
         nc.sync.dma_start(out=ets_win[0:32, :].bitcast(I32), in_=et_scales.bitcast(I32).rearrange("z f c -> f z c"))
         nc.sync.dma_start(offsets[:], offs)
-        nc.scalar.dma_start(out=et_win[0][:].bitcast(I32), in_=et_words[0].bitcast(I32))
+        nc.scalar.dma_start(
+            out=ht_raw[:].rearrange("p z j q -> p z (j q)"),
+            in_=ht.rearrange("(z p j) q -> p z (j q)", z=2, j=PACK),
+        )
         nc.sync.dma_start(out=eds_win[0:P:8, :].bitcast(I32), in_=ed_scales[0].bitcast(I32))
         nc.scalar.activation(warm_out[:], warm_in[:], ACT.Exp)
         nc.sync.dma_start(out=l1_sb[:], in_=l1)
         nc.gpsimd.dma_start(out=l2_sb[:], in_=l2)
-        nc.sync.dma_start(
-            out=ht_raw[:].rearrange("p z j q -> p z (j q)"),
-            in_=ht.rearrange("(z p j) q -> p z (j q)", z=2, j=PACK),
-        )
+        nc.sync.dma_start(out=et_win[0][:].bitcast(I32), in_=et_words[0].bitcast(I32))
         nc.sync.dma_start(out=et_win[1][:].bitcast(I32), in_=et_words[1].bitcast(I32))
         nc.sync.dma_start(
             out=hd_raw[:].rearrange("p j q -> p (j q)"),
@@ -90,17 +90,17 @@ def tile_attend_speculate_residual_kernel(tc, ht, hd, et_words, et_scales, ed_wo
         ets_p = keep.tile([P, 2 * I], U8, name="ets_p", align_bytes=64)
         for q in range(4):
             nc.scalar.dma_start(out=ets_p[32 * q : 32 * q + 4, :].bitcast(I32), in_=ets_g[8 * q : 8 * q + 8, :].bitcast(I32))
-        nc.vector.tensor_copy(et_g[0][:], et_win[0][:].indirect(offsets[:]))
         for z in range(2):
             nc.scalar.copy(out=ht_bf[:, z], in_=ht_raw[:, z].rearrange("p j q -> p q j"))
         nc.vector.tensor_copy(eds_g[:], eds_win[:].indirect(offsets[:]))
         eds_p = keep.tile([P, I], U8, name="eds_p", align_bytes=64)
         for r in range(4):
             nc.sync.dma_start(out=eds_p[r:P:32, :].bitcast(I32), in_=eds_g[8 * r : P : 32, :].bitcast(I32))
-        nc.vector.tensor_copy(et_g[1][:], et_win[1][:].indirect(offsets[:]))
+        nc.vector.tensor_copy(et_g[0][:], et_win[0][:].indirect(offsets[:]))
         nc.vector.quantize_mx(
             out=ht_c[:].bitcast(FP8X4), scales=ht_s[:], in_=ht_bf[:].rearrange("p z q j -> p (z q j)")
         )
+        nc.vector.tensor_copy(et_g[1][:], et_win[1][:].indirect(offsets[:]))
         nc.scalar.copy(out=hd_bf[:], in_=hd_raw[:].rearrange("p j q -> p q j"))
         nl = keep.tile([P, 2], F32, name="nl", tag="hd_raw", align_bytes=64)
         nc.scalar.activation(nl[:, 0:1], l1_sb[:], ACT.Copy, scale=-1.0, bias=-math.log(I))

@@ -21,6 +21,7 @@ P = 128
 PACK = 4
 HALF = I // 2
 PAD = 8
+SPLIT = 160
 
 
 def tile_attend_speculate_residual_kernel(tc, ht, hd, et_words, et_scales, ed_words, ed_scales, l1, l2, offs, out):
@@ -35,7 +36,7 @@ def tile_attend_speculate_residual_kernel(tc, ht, hd, et_words, et_scales, ed_wo
         ets_win = keep.tile([P, T], U8, name="ets_win", align_bytes=64)
         eds_win = keep.tile([P, T], U8, name="eds_win", align_bytes=64)
         et_g = [keep.tile([P, I], U16, name=f"et_g{z}", align_bytes=64) for z in range(2)]
-        ed_g = [keep.tile([P, HALF], U32, name=f"ed_g{h}", align_bytes=64) for h in range(2)]
+        ed_g = [keep.tile([P, Q], U32, name=f"ed_g{n}", align_bytes=64) for n in range(I // Q)]
         ets_g = keep.tile([P, I], U8, name="ets_g", align_bytes=64)
         eds_g = keep.tile([P, I], U8, name="eds_g", align_bytes=64)
         ht_raw = keep.tile([P, 2, PACK, Q], F32, name="ht_raw", tag="ht_raw", align_bytes=64)
@@ -55,12 +56,11 @@ def tile_attend_speculate_residual_kernel(tc, ht, hd, et_words, et_scales, ed_wo
         dd = keep.tile([P, I], F32, name="dd", align_bytes=64)
         low = [keep.tile([P, HALF + PAD], F32, name=f"low{h}", align_bytes=64) for h in range(2)]
         ea_sum = keep.tile([P, I // Q], F32, name="ea_sum")
-        yy = [keep.tile([P, HALF], F32, name=f"yy{h}", align_bytes=64) for h in range(2)]
+        yy = [keep.tile([P, w], F32, name=f"yy{h}", align_bytes=64) for h, w in enumerate((SPLIT, I - SPLIT))]
         ss = keep.tile([P, 1], F32, name="ss")
         rr = keep.tile([P, 1], F32, name="rr")
         a_ps = [psum.tile([P, Q], F32, name=f"a_ps{n}") for n in range(I // Q)]
-        pieces = [(h, lo, lo + HALF // 2) for h in range(2) for lo in (0, HALF // 2)]
-        b_ps = [psum.tile([P, hi - lo], F32, name=f"b_ps{n}") for n, (h, lo, hi) in enumerate(pieces)]
+        b_ps = [psum.tile([P, Q], F32, name=f"b_ps{n}") for n in range(I // Q)]
 
         nc.vector.memset(eds_win[:].bitcast(I32), 0)
         nc.vector.memset(warm_in[:], 0.0)
@@ -75,7 +75,7 @@ def tile_attend_speculate_residual_kernel(tc, ht, hd, et_words, et_scales, ed_wo
             out=ht_raw[:].rearrange("p z j q -> p z (j q)"),
             in_=ht.rearrange("(z p j) q -> p z (j q)", z=2, j=PACK),
         )
-        nc.sync.dma_start(out=eds_win[0:P:8, :].bitcast(I32), in_=ed_scales[0].bitcast(I32))
+        nc.sync.dma_start(out=eds_win[4:P:8, :].bitcast(I32), in_=ed_scales[0].bitcast(I32))
         nc.scalar.activation(warm_out[:], warm_in[:], ACT.Exp)
         nc.sync.dma_start(out=l1_sb[:], in_=l1)
         nc.gpsimd.dma_start(out=l2_sb[:], in_=l2)
@@ -95,7 +95,7 @@ def tile_attend_speculate_residual_kernel(tc, ht, hd, et_words, et_scales, ed_wo
         nc.vector.tensor_copy(eds_g[:], eds_win[:].indirect(offsets[:]))
         eds_p = keep.tile([P, I], U8, name="eds_p", align_bytes=64)
         for r in range(4):
-            nc.sync.dma_start(out=eds_p[r:P:32, :].bitcast(I32), in_=eds_g[8 * r : P : 32, :].bitcast(I32))
+            nc.sync.dma_start(out=eds_p[4 + r : P : 32, :].bitcast(I32), in_=eds_g[4 + 8 * r : P : 32, :].bitcast(I32))
         nc.vector.tensor_copy(et_g[0][:], et_win[0][:].indirect(offsets[:]))
         nc.vector.quantize_mx(
             out=ht_c[:].bitcast(FP8X4), scales=ht_s[:], in_=ht_bf[:].rearrange("p z q j -> p (z q j)")
@@ -125,16 +125,16 @@ def tile_attend_speculate_residual_kernel(tc, ht, hd, et_words, et_scales, ed_wo
             )
         nc.scalar.mul(ea[:, PAD - I // Q : PAD], ea_sum[:], -1.0)
 
-        for h in range(2):
-            nc.vector.tensor_copy(ed_g[h][:], ed_win[:].indirect(offsets[:, h * HALF // 16 : (h + 1) * HALF // 16]))
-        for n, (h, lo, hi) in enumerate(pieces):
-            cols = slice(h * HALF + lo, h * HALF + hi)
+        for n in range(I // Q):
+            nc.vector.tensor_copy(ed_g[n][:], ed_win[:].indirect(offsets[:, n * Q // 16 : (n + 1) * Q // 16]))
+        for n in range(I // Q):
+            cols = slice(n * Q, (n + 1) * Q)
             nc.tensor.matmul_mx(
                 out=b_ps[n][:],
                 lhsT=hd_c[:].bitcast(FP8X4),
                 lhsT_scale=hd_s[:],
-                rhs=ed_g[h][:, lo:hi].bitcast(FP8X4),
-                rhs_scale=eds_p[:, cols],
+                rhs=ed_g[n][:].bitcast(FP8X4),
+                rhs_scale=eds_p[4:P, cols],
                 start=True,
                 stop=True,
             )
@@ -152,11 +152,10 @@ def tile_attend_speculate_residual_kernel(tc, ht, hd, et_words, et_scales, ed_wo
 
         lesser_sum(0, slice(PAD - I // Q, PAD + HALF), ea[:, PAD + I : PAD + I + 1])
         difference(0, HALF)
-        difference(HALF, HALF + Q)
         lesser_sum(1, slice(PAD + HALF, PAD + I + 1), ss[:])
-        difference(HALF + Q, I)
+        difference(HALF, I)
         nc.vector.reciprocal(rr[:], ss[:])
-        nc.scalar.activation(yy[0][:], dd[:, :HALF], ACT.Relu, scale=rr[:])
-        nc.scalar.dma_start(out=out[:, :HALF], in_=yy[0][:])
-        nc.vector.tensor_scalar(yy[1][:], dd[:, HALF:], rr[:], 0.0, ALU.mult, ALU.max)
-        nc.sync.dma_start(out=out[:, HALF:], in_=yy[1][:])
+        nc.scalar.activation(yy[0][:], dd[:, :SPLIT], ACT.Relu, scale=rr[:])
+        nc.scalar.dma_start(out=out[:, :SPLIT], in_=yy[0][:])
+        nc.vector.tensor_scalar(yy[1][:], dd[:, SPLIT:], rr[:], 0.0, ALU.mult, ALU.max)
+        nc.sync.dma_start(out=out[:, SPLIT:], in_=yy[1][:])

@@ -21,7 +21,7 @@ P = 128
 PACK = 4
 HALF = I // 2
 PAD = 8
-SPLIT = 160
+SPLIT = 256
 
 
 def tile_attend_speculate_residual_kernel(tc, ht, hd, et_words, et_scales, ed_words, ed_scales, l1, l2, offs, out):
@@ -32,8 +32,7 @@ def tile_attend_speculate_residual_kernel(tc, ht, hd, et_words, et_scales, ed_wo
 
         offsets = keep.tile([P, I // 16], U16, name="offsets")
         et_win = [keep.tile([P, T], U16, name=f"et_win{z}", align_bytes=64) for z in range(2)]
-        ed_win = keep.tile([P, T], U32, name="ed_win", align_bytes=64)
-        ets_win = keep.tile([P, T], U8, name="ets_win", align_bytes=64)
+        ets_win = keep.tile([P, T], U8, name="ets_win", tag="ets_win", align_bytes=64)
         eds_win = keep.tile([P, T], U8, name="eds_win", align_bytes=64)
         et_g = [keep.tile([P, I], U16, name=f"et_g{z}", align_bytes=64) for z in range(2)]
         ed_g = [keep.tile([P, Q], U32, name=f"ed_g{n}", align_bytes=64) for n in range(I // Q)]
@@ -85,11 +84,12 @@ def tile_attend_speculate_residual_kernel(tc, ht, hd, et_words, et_scales, ed_wo
             out=hd_raw[:].rearrange("p j q -> p (j q)"),
             in_=hd.rearrange("(p j) q -> p (j q)", j=PACK),
         )
-        nc.sync.dma_start(out=ed_win[:].bitcast(I32), in_=ed_words[0].rearrange("p n t -> p (n t)").bitcast(I32))
         nc.vector.tensor_copy(ets_g[:], ets_win[:].indirect(offsets[:]))
         ets_p = keep.tile([P, 2 * I], U8, name="ets_p", align_bytes=64)
         for q in range(4):
-            nc.scalar.dma_start(out=ets_p[32 * q : 32 * q + 4, :].bitcast(I32), in_=ets_g[8 * q : 8 * q + 8, :].bitcast(I32))
+            nc.sync.dma_start(out=ets_p[32 * q : 32 * q + 4, :].bitcast(I32), in_=ets_g[8 * q : 8 * q + 8, :].bitcast(I32))
+        ed_win = keep.tile([P, T], U32, name="ed_win", tag="ets_win", align_bytes=64)
+        nc.sync.dma_start(out=ed_win[:].bitcast(I32), in_=ed_words[0].rearrange("p n t -> p (n t)").bitcast(I32))
         for z in range(2):
             nc.scalar.copy(out=ht_bf[:, z], in_=ht_raw[:, z].rearrange("p j q -> p q j"))
         nc.vector.tensor_copy(eds_g[:], eds_win[:].indirect(offsets[:]))

@@ -48,8 +48,6 @@ def tile_attend_speculate_residual_kernel(tc, ht, hd, et_words, et_scales, ed_wo
         hd_s = keep.tile([P, Q], U8, name="hd_s", align_bytes=64)
         l1_sb = keep.tile([P, 1], F32, name="l1_sb")
         l2_sb = keep.tile([P, 1], F32, name="l2_sb")
-        warm_in = keep.tile([P, 1], F32, name="warm_in")
-        warm_out = keep.tile([P, 1], F32, name="warm_out")
         ea = keep.tile([P, I + 2 * PAD], F32, name="ea", align_bytes=64)
         eb = keep.tile([P, I + 2 * PAD], F32, name="eb", align_bytes=64)
         dd = keep.tile([P, I], F32, name="dd", align_bytes=64)
@@ -62,7 +60,6 @@ def tile_attend_speculate_residual_kernel(tc, ht, hd, et_words, et_scales, ed_wo
         b_ps = [psum.tile([P, Q], F32, name=f"b_ps{n}") for n in range(I // Q)]
 
         nc.vector.memset(eds_win[:].bitcast(I32), 0)
-        nc.vector.memset(warm_in[:], 0.0)
         nc.vector.memset(ets_win[32:64, :].bitcast(I32), 0)
         nc.vector.memset(ets_win[64:P, :].bitcast(I32), 0)
         nc.vector.memset(eb[:, :PAD], 0.0)
@@ -75,7 +72,6 @@ def tile_attend_speculate_residual_kernel(tc, ht, hd, et_words, et_scales, ed_wo
             in_=ht.rearrange("(z p j) q -> p z (j q)", z=2, j=PACK),
         )
         nc.sync.dma_start(out=eds_win[4:P:8, :].bitcast(I32), in_=ed_scales[0].bitcast(I32))
-        nc.scalar.activation(warm_out[:], warm_in[:], ACT.Exp)
         nc.sync.dma_start(out=l1_sb[:], in_=l1)
         nc.gpsimd.dma_start(out=l2_sb[:], in_=l2)
         nc.sync.dma_start(out=et_win[0][:].bitcast(I32), in_=et_words[0].bitcast(I32))

@@ -71,7 +71,7 @@ def tile_attend_speculate_residual_kernel(tc, ht, hd, et_words, et_scales, ed_wo
             out=ht_raw[:].rearrange("p z j q -> p z (j q)"),
             in_=ht.rearrange("(z p j) q -> p z (j q)", z=2, j=PACK),
         )
-        nc.sync.dma_start(out=eds_win[4:P:8, :].bitcast(I32), in_=ed_scales[0].bitcast(I32))
+        nc.sync.dma_start(out=eds_win[32:96:4, :].bitcast(I32), in_=ed_scales[0].bitcast(I32))
         nc.sync.dma_start(out=l1_sb[:], in_=l1)
         nc.gpsimd.dma_start(out=l2_sb[:], in_=l2)
         nc.sync.dma_start(out=et_win[0][:].bitcast(I32), in_=et_words[0].bitcast(I32))
@@ -82,7 +82,7 @@ def tile_attend_speculate_residual_kernel(tc, ht, hd, et_words, et_scales, ed_wo
         )
         nc.vector.tensor_copy(ets_g[:], ets_win[:].indirect(offsets[:]))
         ets_p = keep.tile([P, 2 * I], U8, name="ets_p", align_bytes=64)
-        for q in range(4):
+        for q in (0, 2, 1, 3):
             nc.sync.dma_start(out=ets_p[32 * q : 32 * q + 4, :].bitcast(I32), in_=ets_g[8 * q : 8 * q + 8, :].bitcast(I32))
         ed_win = keep.tile([P, T], U32, name="ed_win", tag="ets_win", align_bytes=64)
         nc.sync.dma_start(out=ed_win[:].bitcast(I32), in_=ed_words[0].rearrange("p n t -> p (n t)").bitcast(I32))
@@ -91,7 +91,7 @@ def tile_attend_speculate_residual_kernel(tc, ht, hd, et_words, et_scales, ed_wo
         nc.vector.tensor_copy(eds_g[:], eds_win[:].indirect(offsets[:]))
         eds_p = keep.tile([P, I], U8, name="eds_p", align_bytes=64)
         for r in range(4):
-            nc.sync.dma_start(out=eds_p[4 + r : P : 32, :].bitcast(I32), in_=eds_g[4 + 8 * r : P : 32, :].bitcast(I32))
+            nc.sync.dma_start(out=eds_p[4 + r : P : 32, :].bitcast(I32), in_=eds_g[32 + 4 * r : 96 : 16, :].bitcast(I32))
         nc.vector.tensor_copy(et_g[0][:], et_win[0][:].indirect(offsets[:]))
         nc.vector.quantize_mx(
             out=ht_c[:].bitcast(FP8X4), scales=ht_s[:], in_=ht_bf[:].rearrange("p z q j -> p (z q j)")

@@ -34,7 +34,8 @@ def tile_attend_speculate_residual_kernel(tc, ht, hd, et_words, et_scales, ed_wo
         et_win = [keep.tile([P, T], U16, name=f"et_win{z}", align_bytes=64) for z in range(2)]
         ets_win = keep.tile([P, T], U8, name="ets_win", tag="ets_win", align_bytes=64)
         eds_win = keep.tile([P, T], U8, name="eds_win", align_bytes=64)
-        et_g = [keep.tile([P, I], U16, name=f"et_g{z}", align_bytes=64) for z in range(2)]
+        et0_g = keep.tile([P, I], U16, name="et0_g", align_bytes=64)
+        et1_g = [keep.tile([P, HALF], U16, name=f"et1_g{h}", align_bytes=64) for h in range(2)]
         ed_g = [keep.tile([P, Q], U32, name=f"ed_g{n}", align_bytes=64) for n in range(I // Q)]
         ets_g = keep.tile([P, I], U8, name="ets_g", align_bytes=64)
         eds_g = keep.tile([P, I], U8, name="eds_g", align_bytes=64)
@@ -92,27 +93,27 @@ def tile_attend_speculate_residual_kernel(tc, ht, hd, et_words, et_scales, ed_wo
         eds_p = keep.tile([P, I], U8, name="eds_p", align_bytes=64)
         for r in range(4):
             nc.sync.dma_start(out=eds_p[4 + r : P : 32, :].bitcast(I32), in_=eds_g[32 + 4 * r : 96 : 16, :].bitcast(I32))
-        nc.vector.tensor_copy(et_g[0][:], et_win[0][:].indirect(offsets[:]))
+        nc.vector.tensor_copy(et0_g[:], et_win[0][:].indirect(offsets[:]))
         nc.vector.quantize_mx(
             out=ht_c[:].bitcast(FP8X4), scales=ht_s[:], in_=ht_bf[:].rearrange("p z q j -> p (z q j)")
         )
-        nc.vector.tensor_copy(et_g[1][:], et_win[1][:].indirect(offsets[:]))
+        for h in range(2):
+            nc.vector.tensor_copy(et1_g[h][:], et_win[1][:].indirect(offsets[:, h * HALF // 16 : (h + 1) * HALF // 16]))
         nc.scalar.copy(out=hd_bf[:], in_=hd_raw[:].rearrange("p j q -> p q j"))
         nl = keep.tile([P, 2], F32, name="nl", tag="hd_raw", align_bytes=64)
         nc.scalar.activation(nl[:, 0:1], l1_sb[:], ACT.Copy, scale=-1.0, bias=-math.log(I))
         nc.scalar.mul(nl[:, 1:2], l2_sb[:], -1.0)
-        for z in range(2):
-            rows = slice(z * Q, (z + 1) * Q)
-            for n in range(I // Q):
-                cols = slice(n * Q, (n + 1) * Q)
+        for n in range(I // Q):
+            for z, words in ((1, et1_g[n // 2][:, n % 2 * Q : (n % 2 + 1) * Q]), (0, et0_g[:, n * Q : (n + 1) * Q])):
+                rows = slice(z * Q, (z + 1) * Q)
                 nc.tensor.matmul_mx(
                     out=a_ps[n][:],
                     lhsT=ht_c[:, rows].bitcast(FP8X4),
                     lhsT_scale=ht_s[:, rows],
-                    rhs=et_g[z][:, cols].bitcast(FP4X4),
+                    rhs=words.bitcast(FP4X4),
                     rhs_scale=ets_p[:, z * I + n * Q : z * I + (n + 1) * Q],
-                    start=(z == 0),
-                    stop=(z == 1),
+                    start=(z == 1),
+                    stop=(z == 0),
                 )
         nc.vector.quantize_mx(out=hd_c[:].bitcast(FP8X4), scales=hd_s[:], in_=hd_bf[:].rearrange("p q j -> p (q j)"))
         for n in range(I // Q):

import math
from contextlib import ExitStack

import concourse.mybir as mybir

D, K, T, I, Q = 1024, 512, 2048, 512, 128
FLOPS = 2 * Q * I * (D + K)

F32 = mybir.dt.float32
BF16 = mybir.dt.bfloat16
I32 = mybir.dt.int32
U32 = mybir.dt.uint32
U16 = mybir.dt.uint16
U8 = mybir.dt.uint8
FP8X4 = mybir.dt.float8_e4m3fn_x4
FP4X4 = mybir.dt.float4_e2m1fn_x4
ALU = mybir.AluOpType
ACT = mybir.ActivationFunctionType

P = 128
PACK = 4
HALF = I // 2
PAD = 8
SPLIT = 256


def tile_attend_speculate_residual_kernel(tc, ht, hd, et_words, et_scales, ed_words, ed_scales, l1, l2, offs, out):
    nc = tc.nc
    with ExitStack() as ctx:
        keep = ctx.enter_context(tc.tile_pool(name="keep", bufs=1))
        psum = ctx.enter_context(tc.psum_pool(name="psum", bufs=1))

        offsets = keep.tile([P, I // 16], U16, name="offsets")
        et_win = [keep.tile([P, T], U16, name=f"et_win{z}", align_bytes=64) for z in range(2)]
        ets_win = keep.tile([P, T], U8, name="ets_win", tag="ets_win", align_bytes=64)
        eds_win = keep.tile([P, T], U8, name="eds_win", align_bytes=64)
        et0_g = keep.tile([P, I], U16, name="et0_g", align_bytes=64)
        et1_g = [keep.tile([P, HALF], U16, name=f"et1_g{h}", align_bytes=64) for h in range(2)]
        ed_g = [keep.tile([P, Q], U32, name=f"ed_g{n}", align_bytes=64) for n in range(I // Q)]
        ets_g = keep.tile([P, I], U8, name="ets_g", align_bytes=64)
        eds_g = keep.tile([P, I], U8, name="eds_g", align_bytes=64)
        ht_raw = keep.tile([P, 2, PACK, Q], F32, name="ht_raw", tag="ht_raw", align_bytes=64)
        hd_raw = keep.tile([P, PACK, Q], F32, name="hd_raw", tag="hd_raw", align_bytes=64)
        ht_bf = keep.tile([P, 2, Q, PACK], BF16, name="ht_bf", align_bytes=64)
        hd_bf = keep.tile([P, Q, PACK], BF16, name="hd_bf", align_bytes=64)
        ht_c = keep.tile([P, 2 * Q], U32, name="ht_c", align_bytes=64)
        ht_s = keep.tile([P, 2 * Q], U8, name="ht_s", align_bytes=64)
        hd_c = keep.tile([P, Q], U32, name="hd_c", align_bytes=64)
        hd_s = keep.tile([P, Q], U8, name="hd_s", align_bytes=64)
        l1_sb = keep.tile([P, 1], F32, name="l1_sb")
        l2_sb = keep.tile([P, 1], F32, name="l2_sb")
        ea = keep.tile([P, I + 2 * PAD], F32, name="ea", align_bytes=64)
        eb = keep.tile([P, I + 2 * PAD], F32, name="eb", align_bytes=64)
        dd = keep.tile([P, I], F32, name="dd", align_bytes=64)
        low = [keep.tile([P, HALF + PAD], F32, name=f"low{h}", align_bytes=64) for h in range(2)]
        ea_sum = keep.tile([P, I // Q], F32, name="ea_sum")
        yy = [keep.tile([P, w], F32, name=f"yy{h}", align_bytes=64) for h, w in enumerate((SPLIT, I - SPLIT))]
        ss = keep.tile([P, 1], F32, name="ss")
        rr = keep.tile([P, 1], F32, name="rr")
        a_ps = [psum.tile([P, Q], F32, name=f"a_ps{n}") for n in range(I // Q)]
        b_ps = [psum.tile([P, Q], F32, name=f"b_ps{n}") for n in range(I // Q)]

        nc.vector.memset(eds_win[:].bitcast(I32), 0)
        nc.vector.memset(ets_win[32:64, :].bitcast(I32), 0)
        nc.vector.memset(ets_win[64:P, :].bitcast(I32), 0)
        nc.vector.memset(eb[:, :PAD], 0.0)
        nc.vector.memset(eb[:, PAD + I :], 0.0)

        nc.sync.dma_start(out=ets_win[0:32, :].bitcast(I32), in_=et_scales.bitcast(I32).rearrange("z f c -> f z c"))
        nc.sync.dma_start(offsets[:], offs)
        nc.scalar.dma_start(
            out=ht_raw[:].rearrange("p z j q -> p z (j q)"),
            in_=ht.rearrange("(z p j) q -> p z (j q)", z=2, j=PACK),
        )
        nc.sync.dma_start(out=eds_win[32:96:4, :].bitcast(I32), in_=ed_scales[0].bitcast(I32))
        nc.sync.dma_start(out=l1_sb[:], in_=l1)
        nc.gpsimd.dma_start(out=l2_sb[:], in_=l2)
        nc.sync.dma_start(out=et_win[0][:].bitcast(I32), in_=et_words[0].bitcast(I32))
        nc.sync.dma_start(out=et_win[1][:].bitcast(I32), in_=et_words[1].bitcast(I32))
        nc.sync.dma_start(
            out=hd_raw[:].rearrange("p j q -> p (j q)"),
            in_=hd.rearrange("(p j) q -> p (j q)", j=PACK),
        )
        nc.vector.tensor_copy(ets_g[:], ets_win[:].indirect(offsets[:]))
        ets_p = keep.tile([P, 2 * I], U8, name="ets_p", align_bytes=64)
        for q in (0, 2, 1, 3):
            nc.sync.dma_start(out=ets_p[32 * q : 32 * q + 4, :].bitcast(I32), in_=ets_g[8 * q : 8 * q + 8, :].bitcast(I32))
        ed_win = keep.tile([P, T], U32, name="ed_win", tag="ets_win", align_bytes=64)
        nc.sync.dma_start(out=ed_win[:].bitcast(I32), in_=ed_words[0].rearrange("p n t -> p (n t)").bitcast(I32))
        for z in range(2):
            nc.scalar.copy(out=ht_bf[:, z], in_=ht_raw[:, z].rearrange("p j q -> p q j"))
        nc.vector.tensor_copy(eds_g[:], eds_win[:].indirect(offsets[:]))
        eds_p = keep.tile([P, I], U8, name="eds_p", align_bytes=64)
        for r in range(4):
            nc.sync.dma_start(out=eds_p[4 + r : P : 32, :].bitcast(I32), in_=eds_g[32 + 4 * r : 96 : 16, :].bitcast(I32))
        nc.vector.tensor_copy(et0_g[:], et_win[0][:].indirect(offsets[:]))
        nc.vector.quantize_mx(
            out=ht_c[:].bitcast(FP8X4), scales=ht_s[:], in_=ht_bf[:].rearrange("p z q j -> p (z q j)")
        )
        for h in range(2):
            nc.vector.tensor_copy(et1_g[h][:], et_win[1][:].indirect(offsets[:, h * HALF // 16 : (h + 1) * HALF // 16]))
        nc.scalar.copy(out=hd_bf[:], in_=hd_raw[:].rearrange("p j q -> p q j"))
        nl = keep.tile([P, 2], F32, name="nl", tag="hd_raw", align_bytes=64)
        nc.scalar.activation(nl[:, 0:1], l1_sb[:], ACT.Copy, scale=-1.0, bias=-math.log(I))
        nc.scalar.mul(nl[:, 1:2], l2_sb[:], -1.0)
        for n in range(I // Q):
            for z, words in ((1, et1_g[n // 2][:, n % 2 * Q : (n % 2 + 1) * Q]), (0, et0_g[:, n * Q : (n + 1) * Q])):
                rows = slice(z * Q, (z + 1) * Q)
                nc.tensor.matmul_mx(
                    out=a_ps[n][:],
                    lhsT=ht_c[:, rows].bitcast(FP8X4),
                    lhsT_scale=ht_s[:, rows],
                    rhs=words.bitcast(FP4X4),
                    rhs_scale=ets_p[:, z * I + n * Q : z * I + (n + 1) * Q],
                    start=(z == 1),
                    stop=(z == 0),
                )
        nc.vector.quantize_mx(out=hd_c[:].bitcast(FP8X4), scales=hd_s[:], in_=hd_bf[:].rearrange("p q j -> p (q j)"))
        for n in range(I // Q):
            nc.scalar.activation(
                ea[:, PAD + n * Q : PAD + (n + 1) * Q], a_ps[n][:], ACT.Exp, bias=nl[:, 0:1], accum_out=ea_sum[:, n : n + 1]
            )
        nc.scalar.mul(ea[:, PAD - I // Q : PAD], ea_sum[:], -1.0)

        for n in range(I // Q):
            nc.vector.tensor_copy(ed_g[n][:], ed_win[:].indirect(offsets[:, n * Q // 16 : (n + 1) * Q // 16]))
        for n in range(I // Q):
            cols = slice(n * Q, (n + 1) * Q)
            nc.tensor.matmul_mx(
                out=b_ps[n][:],
                lhsT=hd_c[:].bitcast(FP8X4),
                lhsT_scale=hd_s[:],
                rhs=ed_g[n][:].bitcast(FP8X4),
                rhs_scale=eds_p[4:P, cols],
                start=True,
                stop=True,
            )
            nc.scalar.activation(eb[:, PAD + cols.start : PAD + cols.stop], b_ps[n][:], ACT.Exp, bias=nl[:, 1:2])

        def lesser_sum(h, cols, total):
            nc.vector.scalar_tensor_tensor(
                low[h][:, : cols.stop - cols.start], eb[:, cols], 1.0 / I, ea[:, cols], ALU.mult, ALU.min, accum_out=total
            )

        def difference(lo, hi):
            nc.vector.scalar_tensor_tensor(
                dd[:, lo:hi], ea[:, PAD + lo : PAD + hi], -float(I), eb[:, PAD + lo : PAD + hi], ALU.mult, ALU.add
            )

        lesser_sum(0, slice(PAD - I // Q, PAD + HALF), ea[:, PAD + I : PAD + I + 1])
        difference(0, HALF)
        lesser_sum(1, slice(PAD + HALF, PAD + I + 1), ss[:])
        difference(HALF, I)
        nc.vector.reciprocal(rr[:], ss[:])
        nc.scalar.activation(yy[0][:], dd[:, :SPLIT], ACT.Relu, scale=rr[:])
        nc.scalar.dma_start(out=out[:, :SPLIT], in_=yy[0][:])
        nc.vector.tensor_scalar(yy[1][:], dd[:, SPLIT:], rr[:], 0.0, ALU.mult, ALU.max)
        nc.sync.dma_start(out=out[:, SPLIT:], in_=yy[1][:])
